import numpy as np, ml_dtypes
CORES = [6,15,38,47]
N = 4
import mx_ref
BF = ml_dtypes.bfloat16
def entries(a):
    return np.ascontiguousarray(a.T).reshape(-1)
def table(e):
    return np.ascontiguousarray(np.reshape(e, (-1, 16)).T).astype(np.int32)
def cols(t, e):
    v = np.concatenate([t.reshape(128, -1, 4), np.zeros((128, 1, 4), BF)], axis=1)
    return np.ascontiguousarray(v[:, e]).reshape(128, -1)
def cut(t, i, w=512):
    return t[:, w * i:w * i + w]
def f(rng, *shape):
    return mx_ref.flush((rng.standard_normal(shape, dtype=np.float32) * np.exp2(rng.integers(-2, 3, shape[:-1] + (1,)))).astype(BF))
def wide(rng, *shape, cols=0):
    v = rng.standard_normal(shape, dtype=np.float32) * np.exp2(rng.integers(-12, 13, shape)).astype(np.float32)
    if cols: v *= np.repeat(np.exp2(rng.integers(-cols, cols + 1, shape[:-2] + (1, shape[-1] // 4))) * (rng.random(shape[:-2] + (1, shape[-1] // 4)) > 0.0625), 4, axis=-1).astype(np.float32)
    return mx_ref.flush(v.astype(BF))
C, R, CAPP = 256, 3, 64
def lists(rng, full=False, stay=False, fresh=False, one=False):
    sl = np.full((N, R, N, CAPP), -1); pa = rng.integers(0, C, (N, R, C))
    for t in range(R):
        if stay: continue
        for r in range(N):
            for d in range(N):
                if d == r: continue
                n = CAPP if full else rng.integers(0, CAPP + 1)
                sl[r, t, d, rng.permutation(CAPP)[:n]] = rng.integers(0, C, n)
        for d in range(N):
            far = C + np.flatnonzero(sl[:, t, d].reshape(-1) >= 0)
            pa[d, t, rng.permutation(C)[:far.size]] = far
            if full: continue
            if far.size: pa[d, t, rng.integers(0, C, C // 16)] = rng.choice(far, C // 16)
            pa[d, t, rng.permutation(C)[:C // 2 if fresh else C // 8]] = -1
    if fresh: pa[rng.integers(0, N), rng.integers(0, R)] = -1
    if one:
        o, j = rng.integers(0, N), rng.integers(0, C)
        for t in range(R - 1):
            q, c, k = (o + rng.integers(1, N)) % N, rng.integers(0, CAPP), rng.integers(0, C)
            sl[o, t, q, c] = j; pa[q, t, k] = C + o * CAPP + c
            o, j = q, k
        for q in range(N):
            c = rng.integers(0, CAPP)
            if q != o: sl[o, R - 1, q, c] = j
            pa[q, R - 1] = j if q == o else C + o * CAPP + c
    return {"sl": np.stack([table(sl[r]) for r in range(N)]), "pa": np.stack([table(pa[r]) for r in range(N)])}
def setup_inputs(rng):
    return {"x": f(rng, N, 128, 4 * C * (R + 1)), "w": f(rng, N, 128, 512 * (R + 1)), **lists(rng)}
def setup_inputs_stay(rng):
    return {**setup_inputs(rng), **lists(rng, stay=True)}
def setup_inputs_far(rng):
    return {**setup_inputs(rng), **lists(rng, full=True)}
def setup_inputs_one(rng):
    return {**setup_inputs(rng), **lists(rng, one=True)}
def setup_inputs_fresh(rng):
    return {**setup_inputs(rng), **lists(rng, fresh=True)}
def setup_inputs_spread(rng):
    d = setup_inputs(rng); d["x"] = wide(rng, N, 128, 4 * C * (R + 1), cols=8); return d
def check_inputs(d):
    b = []
    s = [entries(d["sl"][r]).reshape(R, N, CAPP) for r in range(N)]
    for r in range(N):
        p = entries(d["pa"][r]).reshape(R, C)
        if s[r].min() < -1 or s[r].max() >= C or (s[r][:, r] != -1).any(): b.append("sl")
        if p.min() < -1 or p.max() >= C + N * CAPP: b.append("pa"); continue
        for t in range(R):
            slots = np.concatenate([s[q][t, r] for q in range(N)])
            if (slots[p[t][p[t] >= C] - C] < 0).any(): b.append("pa"); break
    return b
def reference(x, w, sl, pa):
    s = [entries(sl[r]).reshape(R, N, CAPP) for r in range(N)]
    p = [entries(pa[r]).reshape(R, C) for r in range(N)]
    cache = [np.ascontiguousarray(cut(x[r], 0, 4 * C)) for r in range(N)]
    y = np.zeros((N, 128, C * (R + 1)), np.float32)
    for t in range(R + 1):
        if t > 0:
            after = []
            for r in range(N):
                slots = [cols(cache[q], s[q][t - 1, r]) for q in range(N)]
                every = np.concatenate([cache[r]] + slots + [cut(x[r], t, 4 * C)], axis=1)
                v = p[r][t - 1]
                after.append(cols(every, np.where(v < 0, C + N * CAPP + np.arange(C), v)))
            cache = after
        for r in range(N):
            y[r][:, C * t:C * t + C] = mx_ref.matmul(mx_ref.quantize(np.ascontiguousarray(cut(w[r], t))), mx_ref.quantize(cache[r]))
    return {"y": y}

@@ -1,0 +1,297 @@
+from concourse.bass import DstId, RemoteDMATransfer
+from concourse.mybir import dt, AluOpType, ActivationFunctionType
+
+C = 256
+CAP = 64
+LAND = 3 * CAP
+NEW = C + 4 * CAP
+WIN = NEW + C
+F8, U8 = "float8_e4m3fn_x4", "uint8"
+GATES = {0: ["x2", "x3", "w3"], 1: ["w0"], 2: ["w1", "w2"]}
+LATE = ["w3", "w0", "x3", "w1", "w2"]
+NSC = 5
+
+SCRATCH = {
+    "xb": ("sbuf", [128, 4096], "bfloat16"),
+    "wb": ("sbuf", [128, 2048], "bfloat16"),
+    "a0q": ("sbuf", [128, C], F8), "a0s": ("sbuf", [128, C], U8),
+    "wq": ("sbuf", [128, 512], F8), "ws": ("sbuf", [128, 512], U8),
+    "sli": ("sbuf", [128, 48], "int32"), "pai": ("sbuf", [128, 48], "int32"),
+    "ipart": ("sbuf", [128, 1], "int32"), "irep": ("sbuf", [128, 34], "int32"), "icol": ("sbuf", [128, 48], "int32"),
+    "ibit": ("sbuf", [128, 3], "int32"), "fbit": ("sbuf", [128, 3], "float32"),
+    "jneg": ("sbuf", [128, 48], "float32"), "offrep": ("sbuf", [128, 16], "uint16"),
+    "offdup": ("sbuf", [128, 2], "uint16"), "offs": ("sbuf", [128, 16], "uint16"),
+    "dup": ("sbuf", [128, 32], "uint16"), "newp": ("sbuf", [128, 48], "float32"),
+    "mf": ("sbuf", [128, 48], "float32"), "offm": ("sbuf", [128, 48], "uint16"),
+    "yo": ("sbuf", [128, 1024], "float32"), "yw": ("sbuf", [128, WIN], "float32"),
+    "ps": ("psum", [128, 512 * 7], "float32"),
+}
+SEMAPHORES = ["x0a", "x0b", "x1", "x2", "x3", "w0", "w1", "w2", "w3", "sl_in", "pa_in", "iop", "ior", "ioc", "vc", "cst",
+              "ofs", "om", "mf", "dup", "qa", "qx0", "qx1", "qx2", "qx3", "qw0", "qw1", "qw2", "qw3",
+              "kc1", "kc2", "kp1", "kp2", "m0", "m1", "m2", "m3", "m3n", "m3l", "m3m",
+              "e0", "e1", "e2", "e3", "e3l", "fin", "stored"]
+for _t in (1, 2, 3):
+    SCRATCH["w%dq" % _t] = ("sbuf", [128, WIN], F8)
+    SCRATCH["w%ds" % _t] = ("sbuf", [128, WIN], U8)
+    SCRATCH["s%dq" % _t] = ("sbuf", [128, LAND], F8)
+    SCRATCH["s%ds" % _t] = ("sbuf", [128, LAND], U8)
+    SEMAPHORES += [n % _t for n in ("pca%d", "pcb%d", "ppa%d", "ppb%d", "lc%d", "lp%d", "leftc%d", "leftp%d")]
+    if _t > 1:
+        SCRATCH["rg%d" % _t] = ("sbuf", [128, C], "float32")
+        SCRATCH["tr%d" % _t] = ("sbuf", [128, C], "float32")
+        SCRATCH["gg%d" % _t] = ("sbuf", [128, LAND], "float32")
+        SCRATCH["gt%d" % _t] = ("sbuf", [128, LAND], "float32")
+        SCRATCH["off%d" % _t] = ("sbuf", [128, 12], "uint16")
+        SEMAPHORES += [n % _t for n in ("rg%d", "tr%d", "gg%d", "l%d")]
+
+
+def send_calls(core, ranks, topo):
+    def way(c):
+        a, b = topo.chip(core), topo.chip(c)
+        return 1 if topo.mates(a, b) else 2 if topo.same_plane(a, b) else 0
+    far, a, b = [s for _, s in sorted((way(c), s) for s, c in enumerate(ranks) if c != core)]
+    eng = [e for e in topo.engines(core, ranks[far]) if all(e in topo.engines(core, ranks[s]) for s in (a, b))]
+    return [[(far, eng)], [(a, eng[0::2]), (b, eng[1::2])]]
+
+
+def rank_program(g, core, T, topo):
+    r = T.rank_of(core)
+    if r is None:
+        return
+    v, sc, te, sy, sem = g.vector, g.scalar, g.tensor, g.sync, T.sem
+    Copy = ActivationFunctionType.Copy
+    ranks = list(T.cores)
+    others = [d for d in range(len(ranks)) if d != r]
+    wire = send_calls(core, ranks, topo)
+    far, near = [d for d, _ in wire[0]], sorted(d for d, _ in wire[1])
+    at = lambda d: CAP * others.index(d)
+
+    def spans(ds):
+        out = []
+        for d in ds:
+            if out and out[-1][1] == d:
+                out[-1][1] = d + 1
+            else:
+                out.append([d, d + 1])
+        return out
+
+    kept = spans(others)
+
+    def load(name):
+        k, (buf, src, n) = int(name[1]), ((T.xb, T.x, 1024) if name[0] == "x" else (T.wb, T.w, 512))
+        sy.dma_start(buf[:, n * k:n * k + n], src[:, n * k:n * k + n]).then_inc(sem[name], 16)
+
+    sy.dma_start(T.xb[:, 0:512], T.x[:, 0:512]).then_inc(sem.x0a, 16)
+    for k in range(8):
+        q = sc if k < NSC else sy
+        q.dma_start(T.sli[16 * k:16 * k + 16, :], T.sl[:]).then_inc(sem.sl_in, 16)
+    sy.dma_start(T.xb[:, 512:1024], T.x[:, 512:1024]).then_inc(sem.x0b, 16)
+    for k in range(8):
+        sy.dma_start(T.pai[16 * k:16 * k + 16, :], T.pa[:]).then_inc(sem.pa_in, 16)
+    for name in ["x1"] + GATES[0]:
+        load(name)
+
+    g.iota(T.ipart[:], [[0, 1]], 0, 1).then_inc(sem.iop, 1)
+    g.iota(T.irep[:], [[2, 17], [0, 2]], 0, 0).then_inc(sem.ior, 1)
+    g.iota(T.icol[:], [[0, 3], [-16, 16]], -NEW, 0).then_inc(sem.ioc, 1)
+
+    nv = [0]
+
+    def chain(ins):
+        ins.then_inc(sem.vc, 1)
+        nv[0] += 1
+
+    def settle():
+        v.wait_ge(sem.vc, nv[0])
+
+    v.wait_ge(sem.iop, 1)
+    chain(v.tensor_scalar(T.ibit[:, 0:1], T.ipart[:], 15, None, AluOpType.bitwise_and))
+    chain(v.tensor_scalar(T.ibit[:, 1:2], T.ipart[:], 4, 1, AluOpType.arith_shift_right, AluOpType.bitwise_and))
+    chain(v.tensor_scalar(T.ibit[:, 2:3], T.ipart[:], 14, None, AluOpType.bitwise_and))
+    settle()
+    chain(v.tensor_copy(T.fbit[:], T.ibit[:]))
+    settle()
+    v.wait_ge(sem.ior, 1)
+    chain(v.tensor_scalar(T.offdup[:], T.irep[:, 16:33:16], T.fbit[:, 2:3], T.fbit[:, 1:2], AluOpType.add, AluOpType.add))
+    v.tensor_scalar(T.offrep[:], T.irep[:, 0:16], T.fbit[:, 1:2], None, AluOpType.add).then_inc(sem.cst, 1)
+    v.wait_ge(sem.ioc, 1)
+    chain(v.tensor_scalar(T.jneg[:], T.icol[:], T.fbit[:, 0:1], None, AluOpType.subtract))
+
+    v.wait_ge(sem.x0a, 16)
+    v.quantize_mx(T.a0q[:, 0:128], T.a0s[:, 0:128], T.xb[:, 0:512]).then_inc(sem.qa, 1)
+    v.wait_ge(sem.sl_in, 128)
+    v.tensor_copy(T.offs[:], T.sli[:, 0:16]).then_inc(sem.ofs, 1)
+    v.wait_ge(sem.x0b, 16)
+    v.quantize_mx(T.a0q[:, 128:C], T.a0s[:, 128:C], T.xb[:, 512:1024]).then_inc(sem.qa, 1)
+    settle()
+    for q in (v, sc):
+        q.wait_ge(sem.ofs, 1)
+        q.wait_ge(sem.qa, 2)
+
+    def pick(t, wq, ws, off, col):
+        n = []
+        for ds, k in ((far, "a"), (near, "b")):
+            for d, e in spans(ds):
+                a, b, i, j = at(d), at(d) + CAP * (e - d), col(d), col(d) + 4 * (e - d)
+                v.tensor_copy(T["s%dq" % t][:, a:b].bitcast(dt.uint32),
+                              wq[:].bitcast(dt.uint32).indirect(off[:, i:j])).then_inc(sem["pc%s%d" % (k, t)], 1)
+                sc.activation(T["s%ds" % t][:, a:b], ws[:].indirect(off[:, i:j]), Copy).then_inc(sem["pp%s%d" % (k, t)], 1)
+            n.append(len(spans(ds)))
+        return n
+
+    bits = lambda es: sum(1 << e for e in es)
+    got = sum(len(es) for s, c in enumerate(ranks) if s != r for k in send_calls(c, ranks, topo) for d, es in k if d == r)
+    left = sum(len(es) for k in wire for d, es in k)
+
+    def send(t, picks):
+        for part in ("c", "p"):
+            for moves, k, n in zip(wire, "ab", picks):
+                g.wait_ge(sem["p%s%s%d" % (part, k, t)], n)
+                transfers = []
+                for d, es in moves:
+                    rid, pid, _ = topo.addr(ranks[d])
+                    a, b = at(d), C + CAP * r
+                    if part == "c":
+                        src = T["s%dq" % t][:, a:a + CAP].bitcast(dt.uint8)
+                        dst = T["w%dq" % t][:, b:b + CAP].bitcast(dt.uint8)
+                    else:
+                        src, dst = T["s%ds" % t][:, a:a + CAP], T["w%ds" % t][:, b:b + CAP]
+                    transfers.append(RemoteDMATransfer(dst_ids=[DstId(rid=rid, pnc=pid)], dma_engine_mask=bits(es),
+                                                       remote_sem=sem["l%s%d" % (part, t)], src=src, dst=dst))
+                g.remote_dma_fused(transfers, local_sem=sem["left%s%d" % (part, t)])
+
+    send(1, pick(1, T.a0q, T.a0s, T.offs, lambda d: 4 * d))
+
+    v.tensor_copy(T.dup[:], T.sli[:].indirect(T.offdup[:, 0:2])).then_inc(sem.dup, 1)
+    v.wait_ge(sem.pa_in, 128)
+    chain(v.tensor_tensor(T.newp[:], T.pai[:], T.jneg[:], AluOpType.mult))
+    settle()
+    v.tensor_tensor(T.mf[:], T.pai[:], T.newp[:], AluOpType.max).then_inc(sem.mf, 1)
+    v.quantize_mx(T.w1q[:, 0:C], T.w1s[:, 0:C], T.xb[:, 0:1024]).then_inc(sem.qx0, 1)
+    v.wait_ge(sem.mf, 1)
+    v.tensor_copy(T.offm[:], T.mf[:]).then_inc(sem.om, 1)
+
+    def repeat(t):
+        a = 16 * (t - 2)
+        sc.activation(T["rg%d" % t][:], T.mf[:, a:a + 16].indirect(T.offrep[:, 0:16]), Copy).then_inc(sem["rg%d" % t], 1)
+
+    def flatten(t):
+        v.wait_ge(sem["rg%d" % t], 1)
+        v.transpose(T["tr%d" % t][:], T["rg%d" % t][:]).then_inc(sem["tr%d" % t], 1)
+
+    def through(t):
+        sc.wait_ge(sem["tr%d" % t], 1)
+        for d, e in kept:
+            a, b = at(d), 16 * (t - 2)
+            sc.activation(T["gg%d" % t][:, a:a + CAP * (e - d)], T["tr%d" % t][:].indirect(T.dup[:, b + 4 * d:b + 4 * e]),
+                          Copy).then_inc(sem["gg%d" % t], 1)
+
+    def wrap(t):
+        v.wait_ge(sem["gg%d" % t], len(kept))
+        chain(v.transpose(T["gt%d" % t][:], T["gg%d" % t][:]))
+        settle()
+        v.tensor_copy(T["off%d" % t][:], T["gt%d" % t][:, 0:LAND:16]).then_inc(sem["l%d" % t], 1)
+
+    sc.wait_ge(sem.cst, 1)
+    sc.wait_ge(sem.mf, 1)
+    repeat(2)
+    flatten(2)
+    sc.wait_ge(sem.dup, 1)
+    through(2)
+    repeat(3)
+    v.wait_ge(sem.x1, 16)
+    v.quantize_mx(T.w1q[:, NEW:WIN], T.w1s[:, NEW:WIN], T.xb[:, 1024:2048]).then_inc(sem.qx1, 1)
+    wrap(2)
+
+    for t in (1, 2):
+        sy.wait_ge(sem["leftc%d" % t], left)
+        for name in GATES[t]:
+            load(name)
+
+    for t in (2, 3):
+        u = t - 1
+        wq, ws, off = T["w%dq" % u], T["w%ds" % u], T["off%d" % t]
+        for q, own, landed in ((v, "c", "lc%d"), (sc, "p", "lp%d")):
+            q.wait_ge(sem.qx0 if t == 2 else sem["k%s1" % own], 1)
+            q.wait_ge(sem["qx%d" % u], 1)
+            q.wait_ge(sem["l%d" % t], 1)
+            q.wait_ge(sem[landed % u], got)
+        send(t, pick(t, wq, ws, off, lambda d: at(d) // 16))
+        kq, ks, om = T["w%dq" % t], T["w%ds" % t], T.offm[:, 16 * (t - 2):16 * (t - 1)]
+        v.wait_ge(sem.om, 1)
+        v.tensor_copy(kq[:, 0:C].bitcast(dt.uint32), wq[:].bitcast(dt.uint32).indirect(om)).then_inc(sem["kc%d" % u], 1)
+        sc.wait_ge(sem.om, 1)
+        if t == 2:
+            flatten(3)
+            through(3)
+        sc.activation(ks[:, 0:C], ws[:].indirect(om), Copy).then_inc(sem["kp%d" % u], 1)
+        if t == 2:
+            v.wait_ge(sem.x2, 16)
+            v.quantize_mx(T.w2q[:, NEW:WIN], T.w2s[:, NEW:WIN], T.xb[:, 2048:3072]).then_inc(sem.qx2, 1)
+            wrap(3)
+
+    for name in LATE:
+        k = int(name[1])
+        v.wait_ge(sem[name], 16)
+        if name[0] == "w":
+            v.quantize_mx(T.wq[:, 128 * k:128 * k + 128], T.ws[:, 128 * k:128 * k + 128],
+                          T.wb[:, 512 * k:512 * k + 512]).then_inc(sem["qw%d" % k], 1)
+        else:
+            v.quantize_mx(T.w3q[:, NEW:WIN], T.w3s[:, NEW:WIN], T.xb[:, 3072:4096]).then_inc(sem.qx3, 1)
+
+    def product(t, src, ssrc, a, n, bank, done):
+        te.matmul_mx(T.ps[:, 512 * bank:512 * bank + n], T.wq[:, 128 * t:128 * t + 128], T.ws[:, 128 * t:128 * t + 128],
+                     src[:, a:a + n], ssrc[:, a:a + n], True, True).then_inc(done, 1)
+
+    def ready(*names):
+        for n in names:
+            te.wait_ge(sem[n], 1)
+
+    te.wait_ge(sem.qa, 2)
+    ready("qw0")
+    product(0, T.a0q, T.a0s, 0, C, 0, sem.m0)
+    ready("qw3", "qx3")
+    product(3, T.w3q, T.w3s, NEW, C, 4, sem.m3n)
+    ready("qw1", "kc1", "kp1")
+    product(1, T.w2q, T.w2s, 0, C, 1, sem.m1)
+    ready("kc2", "kp2")
+    product(3, T.w3q, T.w3s, 0, C, 3, sem.m3)
+    ready("qw2")
+    product(2, T.w3q, T.w3s, 0, C, 2, sem.m2)
+    for b in (0, 1):
+        sc.wait_ge(sem["m%d" % b], 1)
+        sc.activation(T.yo[:, C * b:C * b + C], T.ps[:, 512 * b:512 * b + C], Copy).then_inc(sem["e%d" % b], 1)
+    sc.wait_ge(sem.m3, 1)
+    sc.activation(T.yw[:, 0:C], T.ps[:, 512 * 3:512 * 3 + C], Copy).then_inc(sem.e3, 1)
+    v.wait_ge(sem.m3n, 1)
+    v.tensor_copy(T.yw[:, NEW:WIN], T.ps[:, 512 * 4:512 * 4 + C]).then_inc(sem.e3, 1)
+    v.wait_ge(sem.m2, 1)
+    v.tensor_copy(T.yo[:, 2 * C:3 * C], T.ps[:, 512 * 2:512 * 2 + C]).then_inc(sem.e2, 1)
+    sy.wait_ge(sem.leftc3, left)
+    for b in (0, 1, 2):
+        sy.wait_ge(sem["e%d" % b], 1)
+        sy.dma_start(T.y[:, C * b:C * b + C], T.yo[:, C * b:C * b + C]).then_inc(sem.stored, 16)
+
+    te.wait_ge(sem.lc3, got)
+    te.wait_ge(sem.lp3, got)
+    for i, (d, e) in enumerate(kept):
+        a, n = C + CAP * d, max(128, CAP * (e - d))
+        skip = CAP if CAP * (e - d) < 128 and d == 0 else 0
+        product(3, T.w3q, T.w3s, a - skip, n, 5 + i, sem.m3m if i else sem.m3l)
+        src, dst = T.ps[:, 512 * (5 + i) + skip:512 * (5 + i) + skip + CAP * (e - d)], T.yw[:, a:C + CAP * e]
+        if i:
+            sc.wait_ge(sem.m3m, 1)
+            sc.activation(dst, src, Copy).then_inc(sem.e3l, 1)
+        else:
+            v.wait_ge(sem.m3l, 1)
+            v.tensor_copy(dst, src).then_inc(sem.e3l, 1)
+    for q in (v, sc):
+        q.wait_ge(sem.e3, 2)
+        q.wait_ge(sem.e3l, len(kept))
+    v.tensor_copy(T.yo[:, 3 * C + 128:4 * C], T.yw[:].indirect(T.offm[:, 40:48])).then_inc(sem.fin, 1)
+    sc.activation(T.yo[:, 3 * C:3 * C + 128], T.yw[:].indirect(T.offm[:, 32:40]), Copy).then_inc(sem.fin, 1)
+    sy.wait_ge(sem.fin, 2)
+    sy.dma_start(T.y[:, 3 * C:4 * C], T.yo[:, 3 * C:4 * C]).then_inc(sem.stored, 16)
+    for t in (1, 2, 3):
+        sy.wait_ge(sem["leftp%d" % t], left)
+    sy.wait_ge(sem.stored, 64)

@@ -7,51 +7,68 @@ LAND = 3 * CAP
 NEW = C + 4 * CAP
 WIN = NEW + C
 F8, U8 = "float8_e4m3fn_x4", "uint8"
-GATES = {0: ["x2", "x3", "w3"], 1: ["w0"], 2: ["w1", "w2"]}
-LATE = ["w3", "w0", "x3", "w1", "w2"]
+GATES = {"": ["x1", "x23", "w3"], "cb1": ["w01"], "cc2": ["w2"]}
+STORES = [(0, 1), (2,)]
 NSC = 5
+PICKS = ["a", "bc"]
 
 SCRATCH = {
     "xb": ("sbuf", [128, 4096], "bfloat16"),
     "wb": ("sbuf", [128, 2048], "bfloat16"),
     "a0q": ("sbuf", [128, C], F8), "a0s": ("sbuf", [128, C], U8),
     "wq": ("sbuf", [128, 512], F8), "ws": ("sbuf", [128, 512], U8),
-    "sli": ("sbuf", [128, 48], "int32"), "pai": ("sbuf", [128, 48], "int32"),
-    "ipart": ("sbuf", [128, 1], "int32"), "irep": ("sbuf", [128, 34], "int32"), "icol": ("sbuf", [128, 48], "int32"),
+    "tab": ("sbuf", [128, 96], "int32"),
+    "ipart": ("sbuf", [128, 1], "int32"), "irep": ("sbuf", [128, 2], "int32"), "icol": ("sbuf", [128, 48], "int32"),
     "ibit": ("sbuf", [128, 3], "int32"), "fbit": ("sbuf", [128, 3], "float32"),
-    "jneg": ("sbuf", [128, 48], "float32"), "offrep": ("sbuf", [128, 16], "uint16"),
-    "offdup": ("sbuf", [128, 2], "uint16"), "offs": ("sbuf", [128, 16], "uint16"),
+    "jneg": ("sbuf", [128, 48], "float32"), "offc": ("sbuf", [128, 2], "uint16"), "offs": ("sbuf", [128, 12], "uint16"),
     "dup": ("sbuf", [128, 32], "uint16"), "newp": ("sbuf", [128, 48], "float32"),
     "mf": ("sbuf", [128, 48], "float32"), "offm": ("sbuf", [128, 48], "uint16"),
+    "rg": ("sbuf", [128, C], "float32"), "tr": ("sbuf", [128, C], "float32"),
     "yo": ("sbuf", [128, 1024], "float32"), "yw": ("sbuf", [128, WIN], "float32"),
     "ps": ("psum", [128, 512 * 7], "float32"),
 }
-SEMAPHORES = ["x0a", "x0b", "x1", "x2", "x3", "w0", "w1", "w2", "w3", "sl_in", "pa_in", "iop", "ior", "ioc", "vc", "cst",
-              "ofs", "om", "mf", "dup", "qa", "qx0", "qx1", "qx2", "qx3", "qw0", "qw1", "qw2", "qw3",
-              "kc1", "kc2", "kp1", "kp2", "m0", "m1", "m2", "m3", "m3n", "m3l", "m3m",
+SEMAPHORES = ["x0a", "x0b", "x1", "x2", "x3", "w0", "w1", "w2", "w3", "sl_in", "pa_in", "iop", "ior", "ioc", "iog", "vc",
+              "ofs", "om", "mf", "dup", "rg", "tr", "qa", "qx0", "qx1", "qx2", "qx3", "qw0", "qw1", "qw2", "qw3",
+              "kc1", "kc2", "kp1", "kp2", "m0", "m1", "m2", "m3", "m3n", "m3f", "m3l", "lpf",
               "e0", "e1", "e2", "e3", "e3l", "fin", "stored"]
 for _t in (1, 2, 3):
     SCRATCH["w%dq" % _t] = ("sbuf", [128, WIN], F8)
     SCRATCH["w%ds" % _t] = ("sbuf", [128, WIN], U8)
     SCRATCH["s%dq" % _t] = ("sbuf", [128, LAND], F8)
     SCRATCH["s%ds" % _t] = ("sbuf", [128, LAND], U8)
-    SEMAPHORES += [n % _t for n in ("pca%d", "pcb%d", "ppa%d", "ppb%d", "lc%d", "lp%d", "leftc%d", "leftp%d")]
+    SEMAPHORES += [n % _t for n in ("pca%d", "pcb%d", "pcc%d", "ppa%d", "ppb%d", "ppc%d", "lc%d", "lp%d",
+                                    "leftca%d", "leftcb%d", "leftcc%d", "leftpa%d", "leftpb%d", "leftpc%d")]
     if _t > 1:
-        SCRATCH["rg%d" % _t] = ("sbuf", [128, C], "float32")
-        SCRATCH["tr%d" % _t] = ("sbuf", [128, C], "float32")
         SCRATCH["gg%d" % _t] = ("sbuf", [128, LAND], "float32")
         SCRATCH["gt%d" % _t] = ("sbuf", [128, LAND], "float32")
         SCRATCH["off%d" % _t] = ("sbuf", [128, 12], "uint16")
-        SEMAPHORES += [n % _t for n in ("rg%d", "tr%d", "gg%d", "l%d")]
+        SEMAPHORES += [n % _t for n in ("gg%d", "l%d")]
 
 
-def send_calls(core, ranks, topo):
+def by_way(core, ranks, topo):
     def way(c):
         a, b = topo.chip(core), topo.chip(c)
         return 1 if topo.mates(a, b) else 2 if topo.same_plane(a, b) else 0
-    far, a, b = [s for _, s in sorted((way(c), s) for s, c in enumerate(ranks) if c != core)]
+    return [s for _, s in sorted((way(c), s) for s, c in enumerate(ranks) if c != core)]
+
+
+def send_calls(core, ranks, topo, t):
+    far, a, b = by_way(core, ranks, topo)
     eng = [e for e in topo.engines(core, ranks[far]) if all(e in topo.engines(core, ranks[s]) for s in (a, b))]
-    return [[(far, eng)], [(a, eng[0::2]), (b, eng[1::2])]]
+    first, second = [(far, eng)], [(a, eng[0::2]), (b, eng[1::2])]
+    calls = {"ca": first, "cb": [(b, eng)], "cc": [(a, eng)], "pa": first}
+    calls.update({"pb": second} if t < 3 else {"pb": [(b, eng)], "pc": [(a, eng)]})
+    return calls
+
+
+def spans(ds):
+    out = []
+    for d in ds:
+        if out and out[-1][1] == d:
+            out[-1][1] = d + 1
+        else:
+            out.append([d, d + 1])
+    return out
 
 
 def rank_program(g, core, T, topo):
@@ -61,39 +78,43 @@ def rank_program(g, core, T, topo):
     v, sc, te, sy, sem = g.vector, g.scalar, g.tensor, g.sync, T.sem
     Copy = ActivationFunctionType.Copy
     ranks = list(T.cores)
-    others = [d for d in range(len(ranks)) if d != r]
-    wire = send_calls(core, ranks, topo)
-    far, near = [d for d, _ in wire[0]], sorted(d for d, _ in wire[1])
-    at = lambda d: CAP * others.index(d)
+    far, near = by_way(core, ranks, topo)[0], sorted(by_way(core, ranks, topo)[1:])
+    side = {moves[0][0]: k[1] for k, moves in send_calls(core, ranks, topo, 1).items() if k[0] == "c"}
+    picks = {grp[0]: [d for d in side if side[d] in grp] for grp in PICKS}
+    side = {d: k for k, ds in picks.items() for d in ds}
+    together = lambda o: all(max(map(o.index, ds)) - min(map(o.index, ds)) < len(ds) for ds in picks.values())
+    order = min((o for o in ([a, b, c] for a in side for b in side for c in side if len({a, b, c}) == 3) if together(o)),
+                key=lambda o: len(spans(o)))
+    at = lambda d: CAP * order.index(d)
+    runs = spans(order)
 
-    def spans(ds):
-        out = []
-        for d in ds:
-            if out and out[-1][1] == d:
-                out[-1][1] = d + 1
-            else:
-                out.append([d, d + 1])
-        return out
-
-    kept = spans(others)
+    def lands(t, d):
+        if t < 3:
+            return C + CAP * r
+        ways = by_way(ranks[d], ranks, topo)
+        return C + CAP * (ways[:1] + sorted(ways[1:])).index(r)
 
     def load(name):
-        k, (buf, src, n) = int(name[1]), ((T.xb, T.x, 1024) if name[0] == "x" else (T.wb, T.w, 512))
-        sy.dma_start(buf[:, n * k:n * k + n], src[:, n * k:n * k + n]).then_inc(sem[name], 16)
+        buf, src, n = (T.xb, T.x, 1024) if name[0] == "x" else (T.wb, T.w, 512)
+        a, b = n * int(name[1]), n * int(name[-1]) + n
+        sy.dma_start(buf[:, a:b], src[:, a:b]).then_inc(sem[name[:2]], 16)
 
+    brought = {name[0] + k: name[:2] for names in GATES.values() for name in names for k in name[1:]}
     sy.dma_start(T.xb[:, 0:512], T.x[:, 0:512]).then_inc(sem.x0a, 16)
     for k in range(8):
         q = sc if k < NSC else sy
-        q.dma_start(T.sli[16 * k:16 * k + 16, :], T.sl[:]).then_inc(sem.sl_in, 16)
+        q.dma_start(T.tab[16 * k:16 * k + 16, 0:48], T.sl[:]).then_inc(sem.sl_in, 16)
     sy.dma_start(T.xb[:, 512:1024], T.x[:, 512:1024]).then_inc(sem.x0b, 16)
     for k in range(8):
-        sy.dma_start(T.pai[16 * k:16 * k + 16, :], T.pa[:]).then_inc(sem.pa_in, 16)
-    for name in ["x1"] + GATES[0]:
+        q = sc if k < 4 else sy
+        q.dma_start(T.tab[16 * k:16 * k + 16, 48:96], T.pa[:]).then_inc(sem.pa_in, 16)
+    for name in GATES[""]:
         load(name)
 
     g.iota(T.ipart[:], [[0, 1]], 0, 1).then_inc(sem.iop, 1)
-    g.iota(T.irep[:], [[2, 17], [0, 2]], 0, 0).then_inc(sem.ior, 1)
+    g.iota(T.irep[:], [[16, 2]], 0, 0).then_inc(sem.ior, 1)
     g.iota(T.icol[:], [[0, 3], [-16, 16]], -NEW, 0).then_inc(sem.ioc, 1)
+    g.iota(T.rg[:], [[0, C]], 0, 0, allow_small_or_imprecise_dtypes=True).then_inc(sem.iog, 1)
 
     nv = [0]
 
@@ -112,101 +133,133 @@ def rank_program(g, core, T, topo):
     chain(v.tensor_copy(T.fbit[:], T.ibit[:]))
     settle()
     v.wait_ge(sem.ior, 1)
-    chain(v.tensor_scalar(T.offdup[:], T.irep[:, 16:33:16], T.fbit[:, 2:3], T.fbit[:, 1:2], AluOpType.add, AluOpType.add))
-    v.tensor_scalar(T.offrep[:], T.irep[:, 0:16], T.fbit[:, 1:2], None, AluOpType.add).then_inc(sem.cst, 1)
+    chain(v.tensor_scalar(T.offc[:], T.irep[:], T.fbit[:, 2:3], T.fbit[:, 1:2], AluOpType.add, AluOpType.add))
     v.wait_ge(sem.ioc, 1)
     chain(v.tensor_scalar(T.jneg[:], T.icol[:], T.fbit[:, 0:1], None, AluOpType.subtract))
 
     v.wait_ge(sem.x0a, 16)
     v.quantize_mx(T.a0q[:, 0:128], T.a0s[:, 0:128], T.xb[:, 0:512]).then_inc(sem.qa, 1)
     v.wait_ge(sem.sl_in, 128)
-    v.tensor_copy(T.offs[:], T.sli[:, 0:16]).then_inc(sem.ofs, 1)
+    for d, e in runs:
+        v.tensor_copy(T.offs[:, at(d) // 16:at(d) // 16 + 4 * (e - d)], T.tab[:, 4 * d:4 * e]).then_inc(sem.ofs, 1)
     v.wait_ge(sem.x0b, 16)
     v.quantize_mx(T.a0q[:, 128:C], T.a0s[:, 128:C], T.xb[:, 512:1024]).then_inc(sem.qa, 1)
     settle()
     for q in (v, sc):
-        q.wait_ge(sem.ofs, 1)
+        q.wait_ge(sem.ofs, len(runs))
         q.wait_ge(sem.qa, 2)
 
-    def pick(t, wq, ws, off, col):
-        n = []
-        for ds, k in ((far, "a"), (near, "b")):
-            for d, e in spans(ds):
-                a, b, i, j = at(d), at(d) + CAP * (e - d), col(d), col(d) + 4 * (e - d)
-                v.tensor_copy(T["s%dq" % t][:, a:b].bitcast(dt.uint32),
-                              wq[:].bitcast(dt.uint32).indirect(off[:, i:j])).then_inc(sem["pc%s%d" % (k, t)], 1)
-                sc.activation(T["s%ds" % t][:, a:b], ws[:].indirect(off[:, i:j]), Copy).then_inc(sem["pp%s%d" % (k, t)], 1)
-            n.append(len(spans(ds)))
-        return n
+    def pick(t, wq, ws, off, sides="abc"):
+        for k, ds in picks.items():
+            if k not in sides:
+                continue
+            a, n = min(map(at, ds)), CAP * len(ds)
+            by = off[:, a // 16:(a + n) // 16]
+            v.tensor_copy(T["s%dq" % t][:, a:a + n].bitcast(dt.uint32),
+                          wq[:].bitcast(dt.uint32).indirect(by)).then_inc(sem["pc%s%d" % (k, t)], 1)
+            sc.activation(T["s%ds" % t][:, a:a + n], ws[:].indirect(by), Copy).then_inc(sem["pp%s%d" % (k, t)], 1)
 
     bits = lambda es: sum(1 << e for e in es)
-    got = sum(len(es) for s, c in enumerate(ranks) if s != r for k in send_calls(c, ranks, topo) for d, es in k if d == r)
-    left = sum(len(es) for k in wire for d, es in k)
+    def got(t, part, senders):
+        return sum(len(es) for s in senders for k, moves in send_calls(ranks[s], ranks, topo, t).items()
+                   for d, es in moves if k[0] == part and d == r)
 
-    def send(t, picks):
-        for part in ("c", "p"):
-            for moves, k, n in zip(wire, "ab", picks):
-                g.wait_ge(sem["p%s%s%d" % (part, k, t)], n)
-                transfers = []
-                for d, es in moves:
-                    rid, pid, _ = topo.addr(ranks[d])
-                    a, b = at(d), C + CAP * r
-                    if part == "c":
-                        src = T["s%dq" % t][:, a:a + CAP].bitcast(dt.uint8)
-                        dst = T["w%dq" % t][:, b:b + CAP].bitcast(dt.uint8)
-                    else:
-                        src, dst = T["s%ds" % t][:, a:a + CAP], T["w%ds" % t][:, b:b + CAP]
-                    transfers.append(RemoteDMATransfer(dst_ids=[DstId(rid=rid, pnc=pid)], dma_engine_mask=bits(es),
-                                                       remote_sem=sem["l%s%d" % (part, t)], src=src, dst=dst))
-                g.remote_dma_fused(transfers, local_sem=sem["left%s%d" % (part, t)])
+    def gone(q, t, k):
+        q.wait_ge(sem["left%s%d" % (k, t)], sum(len(es) for d, es in send_calls(core, ranks, topo, t)[k]))
 
-    send(1, pick(1, T.a0q, T.a0s, T.offs, lambda d: 4 * d))
+    calls_of = lambda t, part: [k for k in send_calls(core, ranks, topo, t) if k[0] == part]
 
-    v.tensor_copy(T.dup[:], T.sli[:].indirect(T.offdup[:, 0:2])).then_inc(sem.dup, 1)
+    def send(t):
+        for k, moves in send_calls(core, ranks, topo, t).items():
+            part, transfers = k[0], []
+            for d, _ in moves:
+                g.wait_ge(sem["p%s%s%d" % (part, side[d], t)], 1)
+            for d, es in moves:
+                rid, pid, _ = topo.addr(ranks[d])
+                a, b = at(d), lands(t, d)
+                if part == "c":
+                    src = T["s%dq" % t][:, a:a + CAP].bitcast(dt.uint8)
+                    dst = T["w%dq" % t][:, b:b + CAP].bitcast(dt.uint8)
+                else:
+                    src, dst = T["s%ds" % t][:, a:a + CAP], T["w%ds" % t][:, b:b + CAP]
+                landed = sem.lpf if (t, part, d) == (3, "p", far) else sem["l%s%d" % (part, t)]
+                transfers.append(RemoteDMATransfer(dst_ids=[DstId(rid=rid, pnc=pid)], dma_engine_mask=bits(es),
+                                                   remote_sem=landed, src=src, dst=dst))
+            g.remote_dma_fused(transfers, local_sem=sem["left%s%d" % (k, t)])
+
+    pick(1, T.a0q, T.a0s, T.offs, "a")
     v.wait_ge(sem.pa_in, 128)
-    chain(v.tensor_tensor(T.newp[:], T.pai[:], T.jneg[:], AluOpType.mult))
+    chain(v.tensor_tensor(T.newp[:], T.tab[:, 48:96], T.jneg[:], AluOpType.mult))
+    pick(1, T.a0q, T.a0s, T.offs, "bc")
     settle()
-    v.tensor_tensor(T.mf[:], T.pai[:], T.newp[:], AluOpType.max).then_inc(sem.mf, 1)
-    v.quantize_mx(T.w1q[:, 0:C], T.w1s[:, 0:C], T.xb[:, 0:1024]).then_inc(sem.qx0, 1)
-    v.wait_ge(sem.mf, 1)
-    v.tensor_copy(T.offm[:], T.mf[:]).then_inc(sem.om, 1)
-
-    def repeat(t):
-        a = 16 * (t - 2)
-        sc.activation(T["rg%d" % t][:], T.mf[:, a:a + 16].indirect(T.offrep[:, 0:16]), Copy).then_inc(sem["rg%d" % t], 1)
-
-    def flatten(t):
-        v.wait_ge(sem["rg%d" % t], 1)
-        v.transpose(T["tr%d" % t][:], T["rg%d" % t][:]).then_inc(sem["tr%d" % t], 1)
-
-    def through(t):
-        sc.wait_ge(sem["tr%d" % t], 1)
-        for d, e in kept:
+    v.tensor_tensor(T.mf[:], T.tab[:, 48:96], T.newp[:], AluOpType.max).then_inc(sem.mf, 1)
+    sc.wait_ge(sem.iog, 1)
+    sc.wait_ge(sem.mf, 1)
+    for i in (0, 1):
+        sc.activation(T.rg[:, i:C:16], T.mf[:, 16 * i:16 * i + 16].indirect(T.offc[:, 0:1]), Copy).then_inc(sem.rg, 1)
+    send(1)
+    v.tensor_copy(T.dup[:], T.tab[:, 16:48].indirect(T.offc[:, 0:2])).then_inc(sem.dup, 1)
+    v.wait_ge(sem.rg, 2)
+    v.transpose(T.tr[:], T.rg[:]).then_inc(sem.tr, 1)
+    sc.wait_ge(sem.tr, 1)
+    sc.wait_ge(sem.dup, 1)
+    for t in (2, 3):
+        for d, e in runs:
             a, b = at(d), 16 * (t - 2)
-            sc.activation(T["gg%d" % t][:, a:a + CAP * (e - d)], T["tr%d" % t][:].indirect(T.dup[:, b + 4 * d:b + 4 * e]),
+            sc.activation(T["gg%d" % t][:, a:a + CAP * (e - d)], T.tr[:].indirect(T.dup[:, b + 4 * d:b + 4 * e]),
                           Copy).then_inc(sem["gg%d" % t], 1)
 
     def wrap(t):
-        v.wait_ge(sem["gg%d" % t], len(kept))
+        v.wait_ge(sem["gg%d" % t], len(runs))
         chain(v.transpose(T["gt%d" % t][:], T["gg%d" % t][:]))
         settle()
-        v.tensor_copy(T["off%d" % t][:], T["gt%d" % t][:, 0:LAND:16]).then_inc(sem["l%d" % t], 1)
+        v.tensor_copy(T["off%d" % t][:], T["gt%d" % t][:, t - 2:LAND:16]).then_inc(sem["l%d" % t], 1)
 
-    sc.wait_ge(sem.cst, 1)
-    sc.wait_ge(sem.mf, 1)
-    repeat(2)
-    flatten(2)
-    sc.wait_ge(sem.dup, 1)
-    through(2)
-    repeat(3)
-    v.wait_ge(sem.x1, 16)
-    v.quantize_mx(T.w1q[:, NEW:WIN], T.w1s[:, NEW:WIN], T.xb[:, 1024:2048]).then_inc(sem.qx1, 1)
+    def quantise(name):
+        k = int(name[1])
+        v.wait_ge(sem[brought[name]], 16)
+        if name[0] == "w":
+            v.quantize_mx(T.wq[:, 128 * k:128 * k + 128], T.ws[:, 128 * k:128 * k + 128],
+                          T.wb[:, 512 * k:512 * k + 512]).then_inc(sem["q" + name], 1)
+        else:
+            v.quantize_mx(T["w%dq" % k][:, NEW:WIN], T["w%ds" % k][:, NEW:WIN],
+                          T.xb[:, 1024 * k:1024 * k + 1024]).then_inc(sem["q" + name], 1)
+
+    v.quantize_mx(T.w1q[:, 0:C], T.w1s[:, 0:C], T.xb[:, 0:1024]).then_inc(sem.qx0, 1)
+    quantise("x1")
     wrap(2)
+    v.wait_ge(sem.mf, 1)
+    v.tensor_copy(T.offm[:], T.mf[:]).then_inc(sem.om, 1)
+    wrap(3)
 
     for t in (1, 2):
-        sy.wait_ge(sem["leftc%d" % t], left)
-        for name in GATES[t]:
-            load(name)
+        for k in calls_of(t, "c"):
+            gone(sy, t, k)
+            for name in GATES.get(k + str(t), []):
+                load(name)
+
+    def product(t, src, ssrc, a, n, bank, done, *needs):
+        for name in needs:
+            te.wait_ge(sem[name], 1)
+        te.matmul_mx(T.ps[:, 512 * bank:512 * bank + n], T.wq[:, 128 * t:128 * t + 128], T.ws[:, 128 * t:128 * t + 128],
+                     src[:, a:a + n], ssrc[:, a:a + n], True, True).then_inc(sem[done], 1)
+
+    def fetch(q, dst, bank, made, done, skip=0):
+        n = dst[1].stop - dst[1].start
+        if made:
+            q.wait_ge(sem[made], 1)
+        src = T.ps[:, 512 * bank + skip:512 * bank + skip + n]
+        ins = v.tensor_copy(dst[0][:, dst[1]], src) if q is v else sc.activation(dst[0][:, dst[1]], src, Copy)
+        ins.then_inc(sem[done], 1)
+
+    te.wait_ge(sem.qa, 2)
+    product(3, T.w3q, T.w3s, NEW, C, 4, "m3n", "qw3", "qx3")
+    product(0, T.a0q, T.a0s, 0, C, 0, "m0", "qw0")
+    product(1, T.w2q, T.w2s, 0, C, 1, "m1", "qw1", "kc1", "kp1")
+    te.wait_ge(sem.kc2, 2)
+    te.wait_ge(sem.kp2, 2)
+    product(3, T.w3q, T.w3s, 0, C, 3, "m3")
+    product(2, T.w3q, T.w3s, 0, C, 2, "m2", "qw2")
 
     for t in (2, 3):
         u = t - 1
@@ -215,83 +268,59 @@ def rank_program(g, core, T, topo):
             q.wait_ge(sem.qx0 if t == 2 else sem["k%s1" % own], 1)
             q.wait_ge(sem["qx%d" % u], 1)
             q.wait_ge(sem["l%d" % t], 1)
-            q.wait_ge(sem[landed % u], got)
-        send(t, pick(t, wq, ws, off, lambda d: at(d) // 16))
-        kq, ks, om = T["w%dq" % t], T["w%ds" % t], T.offm[:, 16 * (t - 2):16 * (t - 1)]
-        v.wait_ge(sem.om, 1)
-        v.tensor_copy(kq[:, 0:C].bitcast(dt.uint32), wq[:].bitcast(dt.uint32).indirect(om)).then_inc(sem["kc%d" % u], 1)
-        sc.wait_ge(sem.om, 1)
+            q.wait_ge(sem[landed % u], got(u, own, order))
+        pick(t, wq, ws, off)
+        send(t)
+        kq, ks, kc, kp = T["w%dq" % t], T["w%ds" % t], sem["kc%d" % u], sem["kp%d" % u]
+        om = lambda a, b: T.offm[:, 16 * (t - 2) + a // 16:16 * (t - 2) + b // 16]
+        codes = lambda a, b: v.tensor_copy(kq[:, a:b].bitcast(dt.uint32), wq[:].bitcast(dt.uint32).indirect(om(a, b)))
+        for q in (v, sc):
+            q.wait_ge(sem.om, 1)
         if t == 2:
-            flatten(3)
-            through(3)
-        sc.activation(ks[:, 0:C], ws[:].indirect(om), Copy).then_inc(sem["kp%d" % u], 1)
-        if t == 2:
-            v.wait_ge(sem.x2, 16)
-            v.quantize_mx(T.w2q[:, NEW:WIN], T.w2s[:, NEW:WIN], T.xb[:, 2048:3072]).then_inc(sem.qx2, 1)
-            wrap(3)
-
-    for name in LATE:
-        k = int(name[1])
-        v.wait_ge(sem[name], 16)
-        if name[0] == "w":
-            v.quantize_mx(T.wq[:, 128 * k:128 * k + 128], T.ws[:, 128 * k:128 * k + 128],
-                          T.wb[:, 512 * k:512 * k + 512]).then_inc(sem["qw%d" % k], 1)
+            quantise("w3")
+            quantise("x3")
+            codes(0, C).then_inc(kc, 1)
+            quantise("w0")
+            quantise("x2")
+            sc.activation(ks[:, 0:C], ws[:].indirect(om(0, C)), Copy).then_inc(kp, 1)
+            fetch(sc, (T.yw, slice(NEW, WIN)), 4, "m3n", "e3")
+            fetch(sc, (T.yo, slice(0, C)), 0, "m0", "e0")
         else:
-            v.quantize_mx(T.w3q[:, NEW:WIN], T.w3s[:, NEW:WIN], T.xb[:, 3072:4096]).then_inc(sem.qx3, 1)
+            quantise("w1")
+            codes(0, C // 2).then_inc(kc, 1)
+            codes(C // 2, C).then_inc(kc, 1)
+            sc.activation(ks[:, 0:C // 2], ws[:].indirect(om(0, C // 2)), Copy).then_inc(kp, 1)
+            v.wait_ge(sem.kp1, 1)
+            v.wait_ge(sem.lp2, got(2, "p", order))
+            v.tensor_copy(ks[:, C // 2:C], ws[:].indirect(om(C // 2, C))).then_inc(kp, 1)
+            quantise("w2")
+    fetch(sc, (T.yo, slice(C, 2 * C)), 1, "m1", "e1")
+    fetch(sc, (T.yw, slice(0, C)), 3, "m3", "e3")
+    fetch(v, (T.yo, slice(2 * C, 3 * C)), 2, "m2", "e2")
+    for k in calls_of(3, "c"):
+        gone(sy, 3, k)
+    for blocks in STORES:
+        for b in blocks:
+            sy.wait_ge(sem["e%d" % b], 1)
+        a, b = C * blocks[0], C * blocks[-1] + C
+        sy.dma_start(T.y[:, a:b], T.yo[:, a:b]).then_inc(sem.stored, 16)
 
-    def product(t, src, ssrc, a, n, bank, done):
-        te.matmul_mx(T.ps[:, 512 * bank:512 * bank + n], T.wq[:, 128 * t:128 * t + 128], T.ws[:, 128 * t:128 * t + 128],
-                     src[:, a:a + n], ssrc[:, a:a + n], True, True).then_inc(done, 1)
-
-    def ready(*names):
-        for n in names:
-            te.wait_ge(sem[n], 1)
-
-    te.wait_ge(sem.qa, 2)
-    ready("qw0")
-    product(0, T.a0q, T.a0s, 0, C, 0, sem.m0)
-    ready("qw3", "qx3")
-    product(3, T.w3q, T.w3s, NEW, C, 4, sem.m3n)
-    ready("qw1", "kc1", "kp1")
-    product(1, T.w2q, T.w2s, 0, C, 1, sem.m1)
-    ready("kc2", "kp2")
-    product(3, T.w3q, T.w3s, 0, C, 3, sem.m3)
-    ready("qw2")
-    product(2, T.w3q, T.w3s, 0, C, 2, sem.m2)
-    for b in (0, 1):
-        sc.wait_ge(sem["m%d" % b], 1)
-        sc.activation(T.yo[:, C * b:C * b + C], T.ps[:, 512 * b:512 * b + C], Copy).then_inc(sem["e%d" % b], 1)
-    sc.wait_ge(sem.m3, 1)
-    sc.activation(T.yw[:, 0:C], T.ps[:, 512 * 3:512 * 3 + C], Copy).then_inc(sem.e3, 1)
-    v.wait_ge(sem.m3n, 1)
-    v.tensor_copy(T.yw[:, NEW:WIN], T.ps[:, 512 * 4:512 * 4 + C]).then_inc(sem.e3, 1)
-    v.wait_ge(sem.m2, 1)
-    v.tensor_copy(T.yo[:, 2 * C:3 * C], T.ps[:, 512 * 2:512 * 2 + C]).then_inc(sem.e2, 1)
-    sy.wait_ge(sem.leftc3, left)
-    for b in (0, 1, 2):
-        sy.wait_ge(sem["e%d" % b], 1)
-        sy.dma_start(T.y[:, C * b:C * b + C], T.yo[:, C * b:C * b + C]).then_inc(sem.stored, 16)
-
-    te.wait_ge(sem.lc3, got)
-    te.wait_ge(sem.lp3, got)
-    for i, (d, e) in enumerate(kept):
-        a, n = C + CAP * d, max(128, CAP * (e - d))
-        skip = CAP if CAP * (e - d) < 128 and d == 0 else 0
-        product(3, T.w3q, T.w3s, a - skip, n, 5 + i, sem.m3m if i else sem.m3l)
-        src, dst = T.ps[:, 512 * (5 + i) + skip:512 * (5 + i) + skip + CAP * (e - d)], T.yw[:, a:C + CAP * e]
-        if i:
-            sc.wait_ge(sem.m3m, 1)
-            sc.activation(dst, src, Copy).then_inc(sem.e3l, 1)
-        else:
-            v.wait_ge(sem.m3l, 1)
-            v.tensor_copy(dst, src).then_inc(sem.e3l, 1)
+    te.wait_ge(sem.lc3, got(3, "c", order))
+    te.wait_ge(sem.lpf, got(3, "p", [far]))
+    product(3, T.w3q, T.w3s, C - CAP, 2 * CAP, 5, "m3f")
+    te.wait_ge(sem.lp3, got(3, "p", near))
+    product(3, T.w3q, T.w3s, C + CAP, 2 * CAP, 6, "m3l")
+    fetch(sc, (T.yw, slice(C + CAP * far, C + CAP * far + CAP)), 5, "m3f", "e3l", CAP)
+    for i, (d, e) in enumerate(spans(near)):
+        fetch(v, (T.yw, slice(C + CAP * d, C + CAP * e)), 6, None if i else "m3l", "e3l", CAP * i)
     for q in (v, sc):
         q.wait_ge(sem.e3, 2)
-        q.wait_ge(sem.e3l, len(kept))
+        q.wait_ge(sem.e3l, 1 + len(spans(near)))
     v.tensor_copy(T.yo[:, 3 * C + 128:4 * C], T.yw[:].indirect(T.offm[:, 40:48])).then_inc(sem.fin, 1)
     sc.activation(T.yo[:, 3 * C:3 * C + 128], T.yw[:].indirect(T.offm[:, 32:40]), Copy).then_inc(sem.fin, 1)
     sy.wait_ge(sem.fin, 2)
     sy.dma_start(T.y[:, 3 * C:4 * C], T.yo[:, 3 * C:4 * C]).then_inc(sem.stored, 16)
     for t in (1, 2, 3):
-        sy.wait_ge(sem["leftp%d" % t], left)
-    sy.wait_ge(sem.stored, 64)
+        for k in calls_of(t, "p"):
+            gone(sy, t, k)
+    sy.wait_ge(sem.stored, 16 * (len(STORES) + 1))

from concourse.bass import DstId, RemoteDMATransfer
from concourse.mybir import dt, AluOpType, ActivationFunctionType

C = 256
CAP = 64
LAND = 3 * CAP
NEW = C + 4 * CAP
WIN = NEW + C
F8, U8 = "float8_e4m3fn_x4", "uint8"
GATES = {"": ["x1", "x23", "w3"], "cb1": ["w01"], "cc2": ["w2"]}
STORES = [(0, 1), (2,)]
NSC = 5
PICKS = ["a", "bc"]

SCRATCH = {
    "xb": ("sbuf", [128, 4096], "bfloat16"),
    "wb": ("sbuf", [128, 2048], "bfloat16"),
    "a0q": ("sbuf", [128, C], F8), "a0s": ("sbuf", [128, C], U8),
    "wq": ("sbuf", [128, 512], F8), "ws": ("sbuf", [128, 512], U8),
    "tab": ("sbuf", [128, 96], "int32"),
    "ipart": ("sbuf", [128, 1], "int32"), "irep": ("sbuf", [128, 2], "int32"), "icol": ("sbuf", [128, 48], "int32"),
    "ibit": ("sbuf", [128, 3], "int32"), "fbit": ("sbuf", [128, 3], "float32"),
    "jneg": ("sbuf", [128, 48], "float32"), "offc": ("sbuf", [128, 2], "uint16"), "offs": ("sbuf", [128, 12], "uint16"),
    "dup": ("sbuf", [128, 32], "uint16"), "newp": ("sbuf", [128, 48], "float32"),
    "mf": ("sbuf", [128, 48], "float32"), "offm": ("sbuf", [128, 48], "uint16"),
    "rg": ("sbuf", [128, C], "float32"), "tr": ("sbuf", [128, C], "float32"),
    "yo": ("sbuf", [128, 1024], "float32"), "yw": ("sbuf", [128, WIN], "float32"),
    "ps": ("psum", [128, 512 * 7], "float32"),
}
SEMAPHORES = ["x0a", "x0b", "x1", "x2", "x3", "w0", "w1", "w2", "w3", "sl_in", "pa_in", "iop", "ior", "ioc", "iog", "vc",
              "ofs", "om", "mf", "dup", "rg", "tr", "qa", "qx0", "qx1", "qx2", "qx3", "qw0", "qw1", "qw2", "qw3",
              "kc1", "kc2", "kp1", "kp2", "m0", "m1", "m2", "m3", "m3n", "m3f", "m3l", "lpf",
              "e0", "e1", "e2", "e3", "e3l", "fin", "stored"]
for _t in (1, 2, 3):
    SCRATCH["w%dq" % _t] = ("sbuf", [128, WIN], F8)
    SCRATCH["w%ds" % _t] = ("sbuf", [128, WIN], U8)
    SCRATCH["s%dq" % _t] = ("sbuf", [128, LAND], F8)
    SCRATCH["s%ds" % _t] = ("sbuf", [128, LAND], U8)
    SEMAPHORES += [n % _t for n in ("pca%d", "pcb%d", "pcc%d", "ppa%d", "ppb%d", "ppc%d", "lc%d", "lp%d",
                                    "leftca%d", "leftcb%d", "leftcc%d", "leftpa%d", "leftpb%d", "leftpc%d")]
    if _t > 1:
        SCRATCH["gg%d" % _t] = ("sbuf", [128, LAND], "float32")
        SCRATCH["gt%d" % _t] = ("sbuf", [128, LAND], "float32")
        SCRATCH["off%d" % _t] = ("sbuf", [128, 12], "uint16")
        SEMAPHORES += [n % _t for n in ("gg%d", "l%d")]


def by_way(core, ranks, topo):
    def way(c):
        a, b = topo.chip(core), topo.chip(c)
        return 1 if topo.mates(a, b) else 2 if topo.same_plane(a, b) else 0
    return [s for _, s in sorted((way(c), s) for s, c in enumerate(ranks) if c != core)]


def send_calls(core, ranks, topo, t):
    far, a, b = by_way(core, ranks, topo)
    eng = [e for e in topo.engines(core, ranks[far]) if all(e in topo.engines(core, ranks[s]) for s in (a, b))]
    first, second = [(far, eng)], [(a, eng[0::2]), (b, eng[1::2])]
    calls = {"ca": first, "cb": [(b, eng)], "cc": [(a, eng)], "pa": first}
    calls.update({"pb": second} if t < 3 else {"pb": [(b, eng)], "pc": [(a, eng)]})
    return calls


def spans(ds):
    out = []
    for d in ds:
        if out and out[-1][1] == d:
            out[-1][1] = d + 1
        else:
            out.append([d, d + 1])
    return out


def rank_program(g, core, T, topo):
    r = T.rank_of(core)
    if r is None:
        return
    v, sc, te, sy, sem = g.vector, g.scalar, g.tensor, g.sync, T.sem
    Copy = ActivationFunctionType.Copy
    ranks = list(T.cores)
    far, near = by_way(core, ranks, topo)[0], sorted(by_way(core, ranks, topo)[1:])
    side = {moves[0][0]: k[1] for k, moves in send_calls(core, ranks, topo, 1).items() if k[0] == "c"}
    picks = {grp[0]: [d for d in side if side[d] in grp] for grp in PICKS}
    side = {d: k for k, ds in picks.items() for d in ds}
    together = lambda o: all(max(map(o.index, ds)) - min(map(o.index, ds)) < len(ds) for ds in picks.values())
    order = min((o for o in ([a, b, c] for a in side for b in side for c in side if len({a, b, c}) == 3) if together(o)),
                key=lambda o: len(spans(o)))
    at = lambda d: CAP * order.index(d)
    runs = spans(order)

    def lands(t, d):
        if t < 3:
            return C + CAP * r
        ways = by_way(ranks[d], ranks, topo)
        return C + CAP * (ways[:1] + sorted(ways[1:])).index(r)

    def load(name):
        buf, src, n = (T.xb, T.x, 1024) if name[0] == "x" else (T.wb, T.w, 512)
        a, b = n * int(name[1]), n * int(name[-1]) + n
        sy.dma_start(buf[:, a:b], src[:, a:b]).then_inc(sem[name[:2]], 16)

    brought = {name[0] + k: name[:2] for names in GATES.values() for name in names for k in name[1:]}
    sy.dma_start(T.xb[:, 0:512], T.x[:, 0:512]).then_inc(sem.x0a, 16)
    for k in range(8):
        q = sc if k < NSC else sy
        q.dma_start(T.tab[16 * k:16 * k + 16, 0:48], T.sl[:]).then_inc(sem.sl_in, 16)
    sy.dma_start(T.xb[:, 512:1024], T.x[:, 512:1024]).then_inc(sem.x0b, 16)
    for k in range(8):
        q = sc if k < 4 else sy
        q.dma_start(T.tab[16 * k:16 * k + 16, 48:96], T.pa[:]).then_inc(sem.pa_in, 16)
    for name in GATES[""]:
        load(name)

    g.iota(T.ipart[:], [[0, 1]], 0, 1).then_inc(sem.iop, 1)
    g.iota(T.irep[:], [[16, 2]], 0, 0).then_inc(sem.ior, 1)
    g.iota(T.icol[:], [[0, 3], [-16, 16]], -NEW, 0).then_inc(sem.ioc, 1)
    g.iota(T.rg[:], [[0, C]], 0, 0, allow_small_or_imprecise_dtypes=True).then_inc(sem.iog, 1)

    nv = [0]

    def chain(ins):
        ins.then_inc(sem.vc, 1)
        nv[0] += 1

    def settle():
        v.wait_ge(sem.vc, nv[0])

    v.wait_ge(sem.iop, 1)
    chain(v.tensor_scalar(T.ibit[:, 0:1], T.ipart[:], 15, None, AluOpType.bitwise_and))
    chain(v.tensor_scalar(T.ibit[:, 1:2], T.ipart[:], 4, 1, AluOpType.arith_shift_right, AluOpType.bitwise_and))
    chain(v.tensor_scalar(T.ibit[:, 2:3], T.ipart[:], 14, None, AluOpType.bitwise_and))
    settle()
    chain(v.tensor_copy(T.fbit[:], T.ibit[:]))
    settle()
    v.wait_ge(sem.ior, 1)
    chain(v.tensor_scalar(T.offc[:], T.irep[:], T.fbit[:, 2:3], T.fbit[:, 1:2], AluOpType.add, AluOpType.add))
    v.wait_ge(sem.ioc, 1)
    chain(v.tensor_scalar(T.jneg[:], T.icol[:], T.fbit[:, 0:1], None, AluOpType.subtract))

    v.wait_ge(sem.x0a, 16)
    v.quantize_mx(T.a0q[:, 0:128], T.a0s[:, 0:128], T.xb[:, 0:512]).then_inc(sem.qa, 1)
    v.wait_ge(sem.sl_in, 128)
    for d, e in runs:
        v.tensor_copy(T.offs[:, at(d) // 16:at(d) // 16 + 4 * (e - d)], T.tab[:, 4 * d:4 * e]).then_inc(sem.ofs, 1)
    v.wait_ge(sem.x0b, 16)
    v.quantize_mx(T.a0q[:, 128:C], T.a0s[:, 128:C], T.xb[:, 512:1024]).then_inc(sem.qa, 1)
    settle()
    for q in (v, sc):
        q.wait_ge(sem.ofs, len(runs))
        q.wait_ge(sem.qa, 2)

    def pick(t, wq, ws, off, sides="abc"):
        for k, ds in picks.items():
            if k not in sides:
                continue
            a, n = min(map(at, ds)), CAP * len(ds)
            by = off[:, a // 16:(a + n) // 16]
            v.tensor_copy(T["s%dq" % t][:, a:a + n].bitcast(dt.uint32),
                          wq[:].bitcast(dt.uint32).indirect(by)).then_inc(sem["pc%s%d" % (k, t)], 1)
            sc.activation(T["s%ds" % t][:, a:a + n], ws[:].indirect(by), Copy).then_inc(sem["pp%s%d" % (k, t)], 1)

    bits = lambda es: sum(1 << e for e in es)
    def got(t, part, senders):
        return sum(len(es) for s in senders for k, moves in send_calls(ranks[s], ranks, topo, t).items()
                   for d, es in moves if k[0] == part and d == r)

    def gone(q, t, k):
        q.wait_ge(sem["left%s%d" % (k, t)], sum(len(es) for d, es in send_calls(core, ranks, topo, t)[k]))

    calls_of = lambda t, part: [k for k in send_calls(core, ranks, topo, t) if k[0] == part]

    def send(t):
        for k, moves in send_calls(core, ranks, topo, t).items():
            part, transfers = k[0], []
            for d, _ in moves:
                g.wait_ge(sem["p%s%s%d" % (part, side[d], t)], 1)
            for d, es in moves:
                rid, pid, _ = topo.addr(ranks[d])
                a, b = at(d), lands(t, d)
                if part == "c":
                    src = T["s%dq" % t][:, a:a + CAP].bitcast(dt.uint8)
                    dst = T["w%dq" % t][:, b:b + CAP].bitcast(dt.uint8)
                else:
                    src, dst = T["s%ds" % t][:, a:a + CAP], T["w%ds" % t][:, b:b + CAP]
                landed = sem.lpf if (t, part, d) == (3, "p", far) else sem["l%s%d" % (part, t)]
                transfers.append(RemoteDMATransfer(dst_ids=[DstId(rid=rid, pnc=pid)], dma_engine_mask=bits(es),
                                                   remote_sem=landed, src=src, dst=dst))
            g.remote_dma_fused(transfers, local_sem=sem["left%s%d" % (k, t)])

    pick(1, T.a0q, T.a0s, T.offs, "a")
    v.wait_ge(sem.pa_in, 128)
    chain(v.tensor_tensor(T.newp[:], T.tab[:, 48:96], T.jneg[:], AluOpType.mult))
    pick(1, T.a0q, T.a0s, T.offs, "bc")
    settle()
    v.tensor_tensor(T.mf[:], T.tab[:, 48:96], T.newp[:], AluOpType.max).then_inc(sem.mf, 1)
    sc.wait_ge(sem.iog, 1)
    sc.wait_ge(sem.mf, 1)
    for i in (0, 1):
        sc.activation(T.rg[:, i:C:16], T.mf[:, 16 * i:16 * i + 16].indirect(T.offc[:, 0:1]), Copy).then_inc(sem.rg, 1)
    send(1)
    v.tensor_copy(T.dup[:], T.tab[:, 16:48].indirect(T.offc[:, 0:2])).then_inc(sem.dup, 1)
    v.wait_ge(sem.rg, 2)
    v.transpose(T.tr[:], T.rg[:]).then_inc(sem.tr, 1)
    sc.wait_ge(sem.tr, 1)
    sc.wait_ge(sem.dup, 1)
    for t in (2, 3):
        for d, e in runs:
            a, b = at(d), 16 * (t - 2)
            sc.activation(T["gg%d" % t][:, a:a + CAP * (e - d)], T.tr[:].indirect(T.dup[:, b + 4 * d:b + 4 * e]),
                          Copy).then_inc(sem["gg%d" % t], 1)

    def wrap(t):
        v.wait_ge(sem["gg%d" % t], len(runs))
        chain(v.transpose(T["gt%d" % t][:], T["gg%d" % t][:]))
        settle()
        v.tensor_copy(T["off%d" % t][:], T["gt%d" % t][:, t - 2:LAND:16]).then_inc(sem["l%d" % t], 1)

    def quantise(name):
        k = int(name[1])
        v.wait_ge(sem[brought[name]], 16)
        if name[0] == "w":
            v.quantize_mx(T.wq[:, 128 * k:128 * k + 128], T.ws[:, 128 * k:128 * k + 128],
                          T.wb[:, 512 * k:512 * k + 512]).then_inc(sem["q" + name], 1)
        else:
            v.quantize_mx(T["w%dq" % k][:, NEW:WIN], T["w%ds" % k][:, NEW:WIN],
                          T.xb[:, 1024 * k:1024 * k + 1024]).then_inc(sem["q" + name], 1)

    v.quantize_mx(T.w1q[:, 0:C], T.w1s[:, 0:C], T.xb[:, 0:1024]).then_inc(sem.qx0, 1)
    quantise("x1")
    wrap(2)
    v.wait_ge(sem.mf, 1)
    v.tensor_copy(T.offm[:], T.mf[:]).then_inc(sem.om, 1)
    wrap(3)

    for t in (1, 2):
        for k in calls_of(t, "c"):
            gone(sy, t, k)
            for name in GATES.get(k + str(t), []):
                load(name)

    def product(t, src, ssrc, a, n, bank, done, *needs):
        for name in needs:
            te.wait_ge(sem[name], 1)
        te.matmul_mx(T.ps[:, 512 * bank:512 * bank + n], T.wq[:, 128 * t:128 * t + 128], T.ws[:, 128 * t:128 * t + 128],
                     src[:, a:a + n], ssrc[:, a:a + n], True, True).then_inc(sem[done], 1)

    def fetch(q, dst, bank, made, done, skip=0):
        n = dst[1].stop - dst[1].start
        if made:
            q.wait_ge(sem[made], 1)
        src = T.ps[:, 512 * bank + skip:512 * bank + skip + n]
        ins = v.tensor_copy(dst[0][:, dst[1]], src) if q is v else sc.activation(dst[0][:, dst[1]], src, Copy)
        ins.then_inc(sem[done], 1)

    te.wait_ge(sem.qa, 2)
    product(3, T.w3q, T.w3s, NEW, C, 4, "m3n", "qw3", "qx3")
    product(0, T.a0q, T.a0s, 0, C, 0, "m0", "qw0")
    product(1, T.w2q, T.w2s, 0, C, 1, "m1", "qw1", "kc1", "kp1")
    te.wait_ge(sem.kc2, 2)
    te.wait_ge(sem.kp2, 2)
    product(3, T.w3q, T.w3s, 0, C, 3, "m3")
    product(2, T.w3q, T.w3s, 0, C, 2, "m2", "qw2")

    for t in (2, 3):
        u = t - 1
        wq, ws, off = T["w%dq" % u], T["w%ds" % u], T["off%d" % t]
        for q, own, landed in ((v, "c", "lc%d"), (sc, "p", "lp%d")):
            q.wait_ge(sem.qx0 if t == 2 else sem["k%s1" % own], 1)
            q.wait_ge(sem["qx%d" % u], 1)
            q.wait_ge(sem["l%d" % t], 1)
            q.wait_ge(sem[landed % u], got(u, own, order))
        pick(t, wq, ws, off)
        send(t)
        kq, ks, kc, kp = T["w%dq" % t], T["w%ds" % t], sem["kc%d" % u], sem["kp%d" % u]
        om = lambda a, b: T.offm[:, 16 * (t - 2) + a // 16:16 * (t - 2) + b // 16]
        codes = lambda a, b: v.tensor_copy(kq[:, a:b].bitcast(dt.uint32), wq[:].bitcast(dt.uint32).indirect(om(a, b)))
        for q in (v, sc):
            q.wait_ge(sem.om, 1)
        if t == 2:
            quantise("w3")
            quantise("x3")
            codes(0, C).then_inc(kc, 1)
            quantise("w0")
            quantise("x2")
            sc.activation(ks[:, 0:C], ws[:].indirect(om(0, C)), Copy).then_inc(kp, 1)
            fetch(sc, (T.yw, slice(NEW, WIN)), 4, "m3n", "e3")
            fetch(sc, (T.yo, slice(0, C)), 0, "m0", "e0")
        else:
            quantise("w1")
            codes(0, C // 2).then_inc(kc, 1)
            codes(C // 2, C).then_inc(kc, 1)
            sc.activation(ks[:, 0:C // 2], ws[:].indirect(om(0, C // 2)), Copy).then_inc(kp, 1)
            v.wait_ge(sem.kp1, 1)
            v.wait_ge(sem.lp2, got(2, "p", order))
            v.tensor_copy(ks[:, C // 2:C], ws[:].indirect(om(C // 2, C))).then_inc(kp, 1)
            quantise("w2")
    fetch(sc, (T.yo, slice(C, 2 * C)), 1, "m1", "e1")
    fetch(sc, (T.yw, slice(0, C)), 3, "m3", "e3")
    fetch(v, (T.yo, slice(2 * C, 3 * C)), 2, "m2", "e2")
    for k in calls_of(3, "c"):
        gone(sy, 3, k)
    for blocks in STORES:
        for b in blocks:
            sy.wait_ge(sem["e%d" % b], 1)
        a, b = C * blocks[0], C * blocks[-1] + C
        sy.dma_start(T.y[:, a:b], T.yo[:, a:b]).then_inc(sem.stored, 16)

    te.wait_ge(sem.lc3, got(3, "c", order))
    te.wait_ge(sem.lpf, got(3, "p", [far]))
    product(3, T.w3q, T.w3s, C - CAP, 2 * CAP, 5, "m3f")
    te.wait_ge(sem.lp3, got(3, "p", near))
    product(3, T.w3q, T.w3s, C + CAP, 2 * CAP, 6, "m3l")
    fetch(sc, (T.yw, slice(C + CAP * far, C + CAP * far + CAP)), 5, "m3f", "e3l", CAP)
    for i, (d, e) in enumerate(spans(near)):
        fetch(v, (T.yw, slice(C + CAP * d, C + CAP * e)), 6, None if i else "m3l", "e3l", CAP * i)
    for q in (v, sc):
        q.wait_ge(sem.e3, 2)
        q.wait_ge(sem.e3l, 1 + len(spans(near)))
    v.tensor_copy(T.yo[:, 3 * C + 128:4 * C], T.yw[:].indirect(T.offm[:, 40:48])).then_inc(sem.fin, 1)
    sc.activation(T.yo[:, 3 * C:3 * C + 128], T.yw[:].indirect(T.offm[:, 32:40]), Copy).then_inc(sem.fin, 1)
    sy.wait_ge(sem.fin, 2)
    sy.dma_start(T.y[:, 3 * C:4 * C], T.yo[:, 3 * C:4 * C]).then_inc(sem.stored, 16)
    for t in (1, 2, 3):
        for k in calls_of(t, "p"):
            gone(sy, t, k)
    sy.wait_ge(sem.stored, 16 * (len(STORES) + 1))
